import numpy as np
import ml_dtypes


def mxq(x, axis, fmt="e4m3"):
    dtype, down = {"e4m3": (ml_dtypes.float8_e4m3fn, 7), "e5m2": (ml_dtypes.float8_e5m2, 14)}[fmt]
    v = np.moveaxis(np.asarray(x, np.float32).astype(ml_dtypes.bfloat16).astype(np.float64), axis, -1)
    blocks = v.reshape(v.shape[:-1] + (-1, 32))
    amax = np.abs(blocks).max(-1, keepdims=True)
    byte = np.maximum(np.where(amax > 0, np.frexp(amax)[1] - 1 + 127, 0) - down, 1)
    scale = np.exp2(byte - 127.0)
    codes = (blocks / scale).astype(np.float32).astype(dtype).astype(np.float64)
    return np.moveaxis((codes * scale).reshape(v.shape), -1, axis)


WIDE = False


def mx_kscale(k):
    if not WIDE:
        return np.ones(k)
    levels = np.array([10, -10, 5, -5, 0])
    if k % 512:
        return np.exp2(np.random.permutation(np.resize(levels, k // 32))).repeat(32)
    a = np.empty((k // 512, 16))
    for p in range(k // 512):
        a[p, :8] = np.random.permutation(np.resize(levels, 8))
        for g in range(8):
            far = levels[np.abs(levels - a[p, g]) >= 10]
            a[p, g + 8] = far[np.random.randint(len(far))]
    return np.exp2(a.ravel()).repeat(32)


def f64(x):
    return np.asarray(x).astype(np.float64)


def striped(idx):
    return np.tile(np.asarray(idx).reshape(-1, 16).T, (8, 1)).astype(np.uint16)


def unstriped(offs):
    return offs[:16].T.reshape(-1).astype(np.int64)


E2M1 = np.array([0.0, 0.5, 1.0, 1.5, 2.0, 3.0, 4.0, 6.0, -0.0, -0.5, -1.0, -1.5, -2.0, -3.0, -4.0, -6.0])


def pack_weight(w, fmt):
    k, n = w.shape
    w = f64(np.asarray(w, np.float32).astype(ml_dtypes.bfloat16)).reshape(k // 32, 32, n)
    amax = np.abs(w).max(1)
    if fmt == "e4m3":
        byte = np.frexp(amax)[1] - 1 + 127 - 7
    else:
        mant, ex = np.frexp(amax / 6.0)
        byte = np.where(mant > 0.5, ex, ex - 1) + 127
    byte = np.clip(np.where(amax > 0, byte, 1), 1, 254)
    scaled = (w * np.exp2(127.0 - byte)[:, None, :]).reshape(k, n).astype(np.float32)
    by_word = np.ascontiguousarray(scaled.reshape(k // 512, 128, 4, n).transpose(0, 1, 3, 2))
    if fmt == "e4m3":
        words = by_word.astype(ml_dtypes.float8_e4m3fn).view(np.uint8)
    else:
        c = by_word.astype(ml_dtypes.float4_e2m1fn).view(np.uint8) & 0xF
        words = (c[..., 0::2] | (c[..., 1::2] << 4)).reshape(k // 512, 128, 2 * n)
    return np.ascontiguousarray(words), np.ascontiguousarray(byte.astype(np.uint8).reshape(k // 512, 16, n))


def unpack_weight(words, scales, fmt):
    g, _, n = scales.shape
    words = np.ascontiguousarray(words).reshape(g, 128, n, -1)
    if fmt == "e4m3":
        vals = words.view(ml_dtypes.float8_e4m3fn).astype(np.float64)
    else:
        nib = np.empty((g, 128, n, 4), np.uint8)
        nib[..., 0::2] = words & 0xF
        nib[..., 1::2] = words >> 4
        vals = E2M1[nib]
    vals = vals * np.repeat(np.exp2(scales.astype(np.float64) - 127.0), 8, axis=1)[..., None]
    return vals.transpose(0, 1, 3, 2).reshape(g * 512, n)


def sgn(shape):
    return np.random.uniform(0.5, 2.0, shape) * np.where(np.random.standard_normal(shape) < 0, -1.0, 1.0)


K, T, J, R, O, U, S, E = 512, 1024, 256, 512, 128, 256, 1024, 256


def setup_inputs():
    n = np.random.standard_normal
    idx = np.random.permutation(T)[:J]
    idx2 = np.random.permutation(J)[:O]
    idx3 = np.random.permutation(S)[:U]
    idx4 = np.random.permutation(E)[:O]
    fk = mx_kscale(K)
    fr = mx_kscale(R)
    xtp = pack_weight(n((K, T)) / fk[:, None], "e4m3")
    wp = pack_weight(n((K, R)) * 1 / np.sqrt(K) * fk[:, None], "e2m1")
    vsp = pack_weight(n((R, S)) * 1 / np.sqrt(R) / fr[:, None], "e2m1")
    return {
        "xt_words": xtp[0],
        "xt_scales": xtp[1],
        "w_words": wp[0],
        "w_scales": wp[1],
        "sg": (0.35 * sgn((R, 1))).astype(np.float32),
        "lo": (np.random.uniform(-1.0, 1.0, (R, 1)) + np.log(fr)[:, None]).astype(np.float32),
        "vs_words": vsp[0],
        "vs_scales": vsp[1],
        "su": (np.random.uniform(0.5, 1.6, (U, 1))).astype(np.float32),
        "offs": striped(idx),
        "offs2": striped(idx2),
        "offs3": striped(idx3),
        "offs4": striped(idx4),
    }


def reference(xt_words, xt_scales, w_words, w_scales, sg, lo, vs_words, vs_scales, su, offs, offs2, offs3, offs4):
    idx = unstriped(offs)
    idx2 = unstriped(offs2)
    idx3 = unstriped(offs3)
    idx4 = unstriped(offs4)
    xtu = unpack_weight(xt_words, xt_scales, "e4m3")
    wu = unpack_weight(w_words, w_scales, "e2m1")
    vsu = unpack_weight(vs_words, vs_scales, "e2m1")
    xtidxg = xtu[:, idx]
    a = wu.T @ xtidxg
    hid = np.exp(a[:, idx2] * f64(sg) + f64(lo))
    vsidx3g = vsu[:, idx3]
    hidq = mxq(hid, 0, "e4m3")
    p = vsidx3g.T @ hidq
    y = np.zeros((U, E))
    y[:, idx4] = p * f64(su)
    return y

@@ -1,0 +1,122 @@
+from contextlib import ExitStack
+
+import concourse.mybir as mybir
+
+K, T, J, R, O, U, S, E = 512, 1024, 256, 512, 128, 256, 1024, 256
+FLOPS = 2 * K * R * J + 2 * R * U * O
+
+F32 = mybir.dt.float32
+BF16 = mybir.dt.bfloat16
+I32 = mybir.dt.int32
+U32 = mybir.dt.uint32
+U16 = mybir.dt.uint16
+U8 = mybir.dt.uint8
+FP8X4 = mybir.dt.float8_e4m3fn_x4
+FP4X4 = mybir.dt.float4_e2m1fn_x4
+ACT = mybir.ActivationFunctionType
+
+P = 128
+PACK = 4
+QUADS = 4
+QUAD = 32
+
+
+def tile_list_prototypes_kernel(tc, xt_words, xt_scales, w_words, w_scales, sg, lo, vs_words, vs_scales, su,
+                                   offs, offs2, offs3, offs4, out):
+    nc = tc.nc
+    with ExitStack() as ctx:
+        held = ctx.enter_context(tc.tile_pool(name="held", bufs=1))
+        psum = ctx.enter_context(tc.psum_pool(name="psum", bufs=1))
+
+        offs_sb = held.tile([P, J // 16], U16, name="offs_sb")
+        offs2_sb = held.tile([P, O // 16], U16, name="offs2_sb")
+        offs3_sb = held.tile([P, U // 16], U16, name="offs3_sb")
+        offs4_sb = held.tile([P, O // 16], U16, name="offs4_sb")
+        xt_sb = held.tile([P, T], U32, name="xt_sb", align_bytes=64)
+        xs_sb = held.tile([P, T], U8, name="xs_sb", align_bytes=64)
+        w_sb = held.tile([P, R], U16, name="w_sb", align_bytes=64)
+        ws_sb = held.tile([P, 2 * R], U8, name="ws_sb", align_bytes=64)
+        vs_sb = held.tile([P, S], U16, name="vs_sb", align_bytes=64)
+        vss_sb = held.tile([P, S], U8, name="vss_sb", align_bytes=64)
+        sg_sb = held.tile([P, PACK], F32, name="sg_sb")
+        lo_sb = held.tile([P, PACK], F32, name="lo_sb")
+        su_sb = held.tile([P, U // P, 1], F32, name="su_sb")
+        pages = [held.tile([P, E], F32, name="page%d" % h) for h in range(U // P)]
+
+        nc.vector.memset(xs_sb[:].bitcast(I32), 0)
+        nc.vector.memset(ws_sb[:].bitcast(I32), 0)
+        nc.vector.memset(vss_sb[:].bitcast(I32), 0)
+        for page in pages:
+            nc.vector.memset(page[:], 0.0)
+
+        def xs_rows(queue, q):
+            queue.dma_start(xs_sb[QUAD * q : QUAD * q + 4, :].bitcast(I32), xt_scales[0, 4 * q : 4 * q + 4, :].bitcast(I32))
+
+        nc.sync.dma_start(offs_sb[:], offs)
+        ws_rows = w_scales[0].bitcast(I32).rearrange("(b a r) c -> a r b c", b=2, a=2)
+        for a in range(2):
+            nc.scalar.dma_start(ws_sb[QUAD * a : QUAD * a + 4, :].bitcast(I32).rearrange("r (b c) -> r b c", b=2), ws_rows[a])
+        for q in range(QUADS):
+            xs_rows(nc.sync if q < 3 else nc.scalar, q)
+        nc.sync.dma_start(xt_sb[:].bitcast(I32), xt_words[0].rearrange("p n t -> p (n t)").bitcast(I32))
+        nc.sync.dma_start(w_sb[:].bitcast(I32), w_words[0].bitcast(I32))
+
+        def vss_rows(queue, q):
+            queue.dma_start(vss_sb[QUAD * q : QUAD * q + 4, :].bitcast(I32), vs_scales[0, 4 * q : 4 * q + 4, :].bitcast(I32))
+
+        nc.gpsimd.dma_start(sg_sb[:], sg.rearrange("(p t) o -> p (t o)", t=PACK))
+        vss_rows(nc.gpsimd, 0)
+        vss_rows(nc.gpsimd, 1)
+        with nc.allow_non_contiguous_dma(reason="one float32 weight a row of out"):
+            nc.gpsimd.dma_start(su_sb[:], su.rearrange("(h p) o -> p h o", p=P))
+
+        nc.sync.dma_start(offs2_sb[:], offs2)
+        nc.sync.dma_start(vs_sb[:].bitcast(I32), vs_words[0].bitcast(I32))
+        vss_rows(nc.sync, 2)
+        vss_rows(nc.sync, 3)
+        nc.sync.dma_start(offs3_sb[:], offs3)
+        nc.sync.dma_start(lo_sb[:], lo.rearrange("(p t) o -> p (t o)", t=PACK))
+        nc.sync.dma_start(offs4_sb[:], offs4)
+
+        ws_words = ws_sb[:].bitcast(I32)
+        nc.vector.tensor_copy(ws_words[64:128, 0 : R // 4], ws_words[0:64, R // 4 : R // 2])
+        ws_dealt = held.tile([P, PACK, P], U8, name="ws_dealt", align_bytes=64)
+        nc.vector.tensor_copy(ws_dealt[:], ws_sb[:, 0:R].rearrange("p (m t) -> p t m", t=PACK))
+        w_dealt = held.tile([P, PACK, P], U16, name="w_dealt", align_bytes=64)
+        w_by_slot = w_sb[:].rearrange("p (m t) -> p t m", t=PACK)
+        nc.scalar.copy(w_dealt[:, 0, :], w_by_slot[:, 0, :])
+        nc.scalar.copy(w_dealt[:, 1:, :], w_by_slot[:, 1:, :])
+
+        xg_scales = held.tile([P, J], U8, name="xg_scales", align_bytes=64)
+        nc.vector.tensor_copy(xg_scales[:], xs_sb[:].indirect(offs_sb[:]))
+        xg_words = held.tile([P, J], U32, name="xg_words", align_bytes=64)
+        nc.vector.tensor_copy(xg_words[:], xt_sb[:].indirect(offs_sb[:]))
+
+        hid = held.tile([P, PACK * O], BF16, name="hid", align_bytes=64)
+        for t in range(PACK):
+            a_ps = psum.tile([P, J], F32, name="a_ps%d" % t)
+            nc.tensor.matmul_mx(a_ps[:], lhsT=w_dealt[:, t, :].bitcast(FP4X4), lhsT_scale=ws_dealt[:, t, :],
+                                rhs=xg_words[:].bitcast(FP8X4), rhs_scale=xg_scales[:], start=True, stop=True)
+            a_sb = held.tile([P, J], F32, name="a_sb%d" % t)
+            nc.vector.tensor_copy(a_sb[:], a_ps[:])
+            nc.scalar.activation(out=hid[:, t : PACK * O : PACK], in_=a_sb[:].indirect(offs2_sb[:]), func=ACT.Exp,
+                                 bias=lo_sb[:, t : t + 1], scale=sg_sb[:, t : t + 1])
+
+        vg_scales = held.tile([P, U], U8, name="vg_scales", align_bytes=64)
+        nc.vector.tensor_copy(vg_scales[:], vss_sb[:].indirect(offs3_sb[:]))
+        vg_words = held.tile([P, U], U16, name="vg_words", align_bytes=64)
+        nc.vector.tensor_copy(vg_words[:], vs_sb[:].indirect(offs3_sb[:]))
+
+        hid_words = held.tile([P, O], U32, name="hid_words", align_bytes=64)
+        hid_scales = held.tile([P, O], U8, name="hid_scales", align_bytes=64)
+        nc.vector.quantize_mx(out=hid_words[:].bitcast(FP8X4), scales=hid_scales[:], in_=hid[:])
+
+        for h, page in enumerate(pages):
+            picks = slice(P * h, P * (h + 1))
+            p_ps = psum.tile([P, O], F32, name="p_ps%d" % h)
+            nc.tensor.matmul_mx(p_ps[:], lhsT=vg_words[:, picks].bitcast(FP4X4), lhsT_scale=vg_scales[:, picks],
+                                rhs=hid_words[:].bitcast(FP8X4), rhs_scale=hid_scales[:], start=True, stop=True)
+            p_sb = held.tile([P, O], F32, name="p_sb%d" % h)
+            nc.vector.tensor_copy(p_sb[:], p_ps[:])
+            nc.scalar.activation(out=page[:].indirect(offs4_sb[:]), in_=p_sb[:], func=ACT.Copy, scale=su_sb[:, h, :])
+            nc.sync.dma_start(out[picks, :], page[:])

@@ -26,6 +26,7 @@ def tile_list_prototypes_kernel(tc, xt_words, xt_scales, w_words, w_scales, sg, 
     nc = tc.nc
     with ExitStack() as ctx:
         held = ctx.enter_context(tc.tile_pool(name="held", bufs=1))
+        shared = ctx.enter_context(tc.tile_pool(name="shared", bufs=1))
         psum = ctx.enter_context(tc.psum_pool(name="psum", bufs=1))
 
         offs_sb = held.tile([P, J // 16], U16, name="offs_sb")
@@ -36,78 +37,90 @@ def tile_list_prototypes_kernel(tc, xt_words, xt_scales, w_words, w_scales, sg, 
         xs_sb = held.tile([P, T], U8, name="xs_sb", align_bytes=64)
         w_sb = held.tile([P, R], U16, name="w_sb", align_bytes=64)
         ws_sb = held.tile([P, 2 * R], U8, name="ws_sb", align_bytes=64)
-        vs_sb = held.tile([P, S], U16, name="vs_sb", align_bytes=64)
-        vss_sb = held.tile([P, S], U8, name="vss_sb", align_bytes=64)
+        vs_sb = shared.tile([P, S], U16, name="vs_sb", offset=0, align_bytes=64)
+        vss_sb = held.tile([P, S], U8, name="vss_sb", tag="vss_then_hid_words", align_bytes=64)
         sg_sb = held.tile([P, PACK], F32, name="sg_sb")
         lo_sb = held.tile([P, PACK], F32, name="lo_sb")
         su_sb = held.tile([P, U // P, 1], F32, name="su_sb")
         pages = [held.tile([P, E], F32, name="page%d" % h) for h in range(U // P)]
 
-        nc.vector.memset(xs_sb[:].bitcast(I32), 0)
         nc.vector.memset(ws_sb[:].bitcast(I32), 0)
-        nc.vector.memset(vss_sb[:].bitcast(I32), 0)
+        nc.gpsimd.dma_start(w_sb[:].bitcast(I32), w_words[0].bitcast(I32))
+        nc.gpsimd.memset(vss_sb[:].bitcast(I32), 0)
         for page in pages:
-            nc.vector.memset(page[:], 0.0)
+            nc.gpsimd.memset(page[:], 0.0)
 
         def xs_rows(queue, q):
-            queue.dma_start(xs_sb[QUAD * q : QUAD * q + 4, :].bitcast(I32), xt_scales[0, 4 * q : 4 * q + 4, :].bitcast(I32))
+            rows = xt_scales[0, 4 * q : 4 * q + 4, :].bitcast(I32)
+            queue.dma_start(xs_sb[QUAD * q : QUAD * (q + 1), :].bitcast(I32), rows.unsqueeze(0).to_broadcast([QUAD // 4, 4, T // 4]))
 
         nc.sync.dma_start(offs_sb[:], offs)
+        for q in range(QUADS):
+            xs_rows(nc.scalar if q < 2 else nc.sync, q)
         ws_rows = w_scales[0].bitcast(I32).rearrange("(b a r) c -> a r b c", b=2, a=2)
         for a in range(2):
-            nc.scalar.dma_start(ws_sb[QUAD * a : QUAD * a + 4, :].bitcast(I32).rearrange("r (b c) -> r b c", b=2), ws_rows[a])
-        for q in range(QUADS):
-            xs_rows(nc.sync if q < 3 else nc.scalar, q)
+            nc.sync.dma_start(ws_sb[QUAD * a : QUAD * a + 4, :].bitcast(I32).rearrange("r (b c) -> r b c", b=2), ws_rows[a])
         nc.sync.dma_start(xt_sb[:].bitcast(I32), xt_words[0].rearrange("p n t -> p (n t)").bitcast(I32))
-        nc.sync.dma_start(w_sb[:].bitcast(I32), w_words[0].bitcast(I32))
 
-        def vss_rows(queue, q):
-            queue.dma_start(vss_sb[QUAD * q : QUAD * q + 4, :].bitcast(I32), vs_scales[0, 4 * q : 4 * q + 4, :].bitcast(I32))
-
-        nc.gpsimd.dma_start(sg_sb[:], sg.rearrange("(p t) o -> p (t o)", t=PACK))
-        vss_rows(nc.gpsimd, 0)
-        vss_rows(nc.gpsimd, 1)
-        with nc.allow_non_contiguous_dma(reason="one float32 weight a row of out"):
-            nc.gpsimd.dma_start(su_sb[:], su.rearrange("(h p) o -> p h o", p=P))
-
-        nc.sync.dma_start(offs2_sb[:], offs2)
         nc.sync.dma_start(vs_sb[:].bitcast(I32), vs_words[0].bitcast(I32))
-        vss_rows(nc.sync, 2)
-        vss_rows(nc.sync, 3)
         nc.sync.dma_start(offs3_sb[:], offs3)
+        nc.sync.dma_start(offs2_sb[:], offs2)
+        nc.sync.dma_start(sg_sb[:], sg.rearrange("(p t) o -> p (t o)", t=PACK))
         nc.sync.dma_start(lo_sb[:], lo.rearrange("(p t) o -> p (t o)", t=PACK))
+        for q in range(QUADS):
+            nc.sync.dma_start(vss_sb[QUAD * q : QUAD * q + 4, :].bitcast(I32), vs_scales[0, 4 * q : 4 * q + 4, :].bitcast(I32))
         nc.sync.dma_start(offs4_sb[:], offs4)
+        with nc.allow_non_contiguous_dma(reason="one float32 weight a row of out"):
+            nc.sync.dma_start(su_sb[:], su.rearrange("(h p) o -> p h o", p=P))
 
         ws_words = ws_sb[:].bitcast(I32)
         nc.vector.tensor_copy(ws_words[64:128, 0 : R // 4], ws_words[0:64, R // 4 : R // 2])
-        ws_dealt = held.tile([P, PACK, P], U8, name="ws_dealt", align_bytes=64)
-        nc.vector.tensor_copy(ws_dealt[:], ws_sb[:, 0:R].rearrange("p (m t) -> p t m", t=PACK))
-        w_dealt = held.tile([P, PACK, P], U16, name="w_dealt", align_bytes=64)
+        ws_dealt = held.tile([P, PACK * P], U8, name="ws_dealt", align_bytes=64)
+        nc.vector.tensor_copy(ws_dealt[:].rearrange("p (t m) -> p t m", t=PACK), ws_sb[:, 0:R].rearrange("p (m t) -> p t m", t=PACK))
         w_by_slot = w_sb[:].rearrange("p (m t) -> p t m", t=PACK)
-        nc.scalar.copy(w_dealt[:, 0, :], w_by_slot[:, 0, :])
-        nc.scalar.copy(w_dealt[:, 1:, :], w_by_slot[:, 1:, :])
+        w_dealt = []
+        for t in range(PACK):
+            slot = held.tile([P, P], U16, name="w_slot%d" % t, align_bytes=64)
+            nc.scalar.copy(slot[:], w_by_slot[:, t, :])
+            w_dealt.append(slot)
 
         xg_scales = held.tile([P, J], U8, name="xg_scales", align_bytes=64)
         nc.vector.tensor_copy(xg_scales[:], xs_sb[:].indirect(offs_sb[:]))
+        halves = [slice(0, J // 2), slice(J // 2, J)]
         xg_words = held.tile([P, J], U32, name="xg_words", align_bytes=64)
-        nc.vector.tensor_copy(xg_words[:], xt_sb[:].indirect(offs_sb[:]))
+        for cols in halves:
+            nc.vector.tensor_copy(xg_words[:, cols], xt_sb[:].indirect(offs_sb[:, cols.start // 16 : cols.stop // 16]))
+
+        vg_words = held.tile([P, U], U16, name="vg_words", align_bytes=64)
+        nc.vector.tensor_copy(vg_words[:], vs_sb[:].indirect(offs3_sb[:]))
 
         hid = held.tile([P, PACK * O], BF16, name="hid", align_bytes=64)
+
+        def product(t, cols, a_ps):
+            nc.tensor.matmul_mx(a_ps, lhsT=w_dealt[t][:].bitcast(FP4X4), lhsT_scale=ws_dealt[:, P * t : P * (t + 1)],
+                                rhs=xg_words[:, cols].bitcast(FP8X4), rhs_scale=xg_scales[:, cols], start=True, stop=True)
+
         for t in range(PACK):
-            a_ps = psum.tile([P, J], F32, name="a_ps%d" % t)
-            nc.tensor.matmul_mx(a_ps[:], lhsT=w_dealt[:, t, :].bitcast(FP4X4), lhsT_scale=ws_dealt[:, t, :],
-                                rhs=xg_words[:].bitcast(FP8X4), rhs_scale=xg_scales[:], start=True, stop=True)
-            a_sb = held.tile([P, J], F32, name="a_sb%d" % t)
-            nc.vector.tensor_copy(a_sb[:], a_ps[:])
+            if t in (1, 2):
+                a_sb = shared.tile([P, J], F32, name="a_sb%d" % t, offset=4 * J * (t - 1), align_bytes=64)
+            else:
+                a_sb = held.tile([P, J], F32, name="a_sb%d" % t, tag="a0_then_a3")
+            if t == 0:
+                for i, cols in enumerate(halves):
+                    a_ps = psum.tile([P, J // 2], F32, name="a_ps0_%d" % i)
+                    product(t, cols, a_ps[:])
+                    nc.scalar.copy(a_sb[:, cols], a_ps[:])
+            else:
+                a_ps = psum.tile([P, J], F32, name="a_ps%d" % t)
+                product(t, slice(0, J), a_ps[:])
+                nc.vector.tensor_copy(a_sb[:], a_ps[:])
             nc.scalar.activation(out=hid[:, t : PACK * O : PACK], in_=a_sb[:].indirect(offs2_sb[:]), func=ACT.Exp,
                                  bias=lo_sb[:, t : t + 1], scale=sg_sb[:, t : t + 1])
 
         vg_scales = held.tile([P, U], U8, name="vg_scales", align_bytes=64)
         nc.vector.tensor_copy(vg_scales[:], vss_sb[:].indirect(offs3_sb[:]))
-        vg_words = held.tile([P, U], U16, name="vg_words", align_bytes=64)
-        nc.vector.tensor_copy(vg_words[:], vs_sb[:].indirect(offs3_sb[:]))
 
-        hid_words = held.tile([P, O], U32, name="hid_words", align_bytes=64)
+        hid_words = held.tile([P, O], U32, name="hid_words", tag="vss_then_hid_words", align_bytes=64)
         hid_scales = held.tile([P, O], U8, name="hid_scales", align_bytes=64)
         nc.vector.quantize_mx(out=hid_words[:].bitcast(FP8X4), scales=hid_scales[:], in_=hid[:])
 

@@ -45,10 +45,9 @@ def tile_list_prototypes_kernel(tc, xt_words, xt_scales, w_words, w_scales, sg, 
         pages = [held.tile([P, E], F32, name="page%d" % h) for h in range(U // P)]
 
         nc.vector.memset(ws_sb[:].bitcast(I32), 0)
-        nc.gpsimd.dma_start(w_sb[:].bitcast(I32), w_words[0].bitcast(I32))
-        nc.gpsimd.memset(vss_sb[:].bitcast(I32), 0)
+        nc.vector.memset(vss_sb[:].bitcast(I32), 0)
         for page in pages:
-            nc.gpsimd.memset(page[:], 0.0)
+            nc.vector.memset(page[:], 0.0)
 
         def xs_rows(queue, q):
             rows = xt_scales[0, 4 * q : 4 * q + 4, :].bitcast(I32)
@@ -56,12 +55,13 @@ def tile_list_prototypes_kernel(tc, xt_words, xt_scales, w_words, w_scales, sg, 
 
         nc.sync.dma_start(offs_sb[:], offs)
         for q in range(QUADS):
-            xs_rows(nc.scalar if q < 2 else nc.sync, q)
+            xs_rows(nc.scalar if q < 3 else nc.sync, q)
         ws_rows = w_scales[0].bitcast(I32).rearrange("(b a r) c -> a r b c", b=2, a=2)
         for a in range(2):
             nc.sync.dma_start(ws_sb[QUAD * a : QUAD * a + 4, :].bitcast(I32).rearrange("r (b c) -> r b c", b=2), ws_rows[a])
-        nc.sync.dma_start(xt_sb[:].bitcast(I32), xt_words[0].rearrange("p n t -> p (n t)").bitcast(I32))
+        nc.scalar.dma_start(xt_sb[:].bitcast(I32), xt_words[0].rearrange("p n t -> p (n t)").bitcast(I32))
 
+        nc.sync.dma_start(w_sb[:].bitcast(I32), w_words[0].bitcast(I32))
         nc.sync.dma_start(vs_sb[:].bitcast(I32), vs_words[0].bitcast(I32))
         nc.sync.dma_start(offs3_sb[:], offs3)
         nc.sync.dma_start(offs2_sb[:], offs2)

from contextlib import ExitStack

import concourse.mybir as mybir

K, T, J, R, O, U, S, E = 512, 1024, 256, 512, 128, 256, 1024, 256
FLOPS = 2 * K * R * J + 2 * R * U * O

F32 = mybir.dt.float32
BF16 = mybir.dt.bfloat16
I32 = mybir.dt.int32
U32 = mybir.dt.uint32
U16 = mybir.dt.uint16
U8 = mybir.dt.uint8
FP8X4 = mybir.dt.float8_e4m3fn_x4
FP4X4 = mybir.dt.float4_e2m1fn_x4
ACT = mybir.ActivationFunctionType

P = 128
PACK = 4
QUADS = 4
QUAD = 32


def tile_list_prototypes_kernel(tc, xt_words, xt_scales, w_words, w_scales, sg, lo, vs_words, vs_scales, su,
                                   offs, offs2, offs3, offs4, out):
    nc = tc.nc
    with ExitStack() as ctx:
        held = ctx.enter_context(tc.tile_pool(name="held", bufs=1))
        shared = ctx.enter_context(tc.tile_pool(name="shared", bufs=1))
        psum = ctx.enter_context(tc.psum_pool(name="psum", bufs=1))

        offs_sb = held.tile([P, J // 16], U16, name="offs_sb")
        offs2_sb = held.tile([P, O // 16], U16, name="offs2_sb")
        offs3_sb = held.tile([P, U // 16], U16, name="offs3_sb")
        offs4_sb = held.tile([P, O // 16], U16, name="offs4_sb")
        xt_sb = held.tile([P, T], U32, name="xt_sb", align_bytes=64)
        xs_sb = held.tile([P, T], U8, name="xs_sb", align_bytes=64)
        w_sb = held.tile([P, R], U16, name="w_sb", align_bytes=64)
        ws_sb = held.tile([P, 2 * R], U8, name="ws_sb", align_bytes=64)
        vs_sb = shared.tile([P, S], U16, name="vs_sb", offset=0, align_bytes=64)
        vss_sb = held.tile([P, S], U8, name="vss_sb", tag="vss_then_hid_words", align_bytes=64)
        sg_sb = held.tile([P, PACK], F32, name="sg_sb")
        lo_sb = held.tile([P, PACK], F32, name="lo_sb")
        su_sb = held.tile([P, U // P, 1], F32, name="su_sb")
        pages = [held.tile([P, E], F32, name="page%d" % h) for h in range(U // P)]

        nc.vector.memset(ws_sb[:].bitcast(I32), 0)
        nc.vector.memset(vss_sb[:].bitcast(I32), 0)
        for page in pages:
            nc.vector.memset(page[:], 0.0)

        def xs_rows(queue, q):
            rows = xt_scales[0, 4 * q : 4 * q + 4, :].bitcast(I32)
            queue.dma_start(xs_sb[QUAD * q : QUAD * (q + 1), :].bitcast(I32), rows.unsqueeze(0).to_broadcast([QUAD // 4, 4, T // 4]))

        nc.sync.dma_start(offs_sb[:], offs)
        for q in range(QUADS):
            xs_rows(nc.scalar if q < 3 else nc.sync, q)
        ws_rows = w_scales[0].bitcast(I32).rearrange("(b a r) c -> a r b c", b=2, a=2)
        for a in range(2):
            nc.sync.dma_start(ws_sb[QUAD * a : QUAD * a + 4, :].bitcast(I32).rearrange("r (b c) -> r b c", b=2), ws_rows[a])
        nc.scalar.dma_start(xt_sb[:].bitcast(I32), xt_words[0].rearrange("p n t -> p (n t)").bitcast(I32))

        nc.sync.dma_start(w_sb[:].bitcast(I32), w_words[0].bitcast(I32))
        nc.sync.dma_start(vs_sb[:].bitcast(I32), vs_words[0].bitcast(I32))
        nc.sync.dma_start(offs3_sb[:], offs3)
        nc.sync.dma_start(offs2_sb[:], offs2)
        nc.sync.dma_start(sg_sb[:], sg.rearrange("(p t) o -> p (t o)", t=PACK))
        nc.sync.dma_start(lo_sb[:], lo.rearrange("(p t) o -> p (t o)", t=PACK))
        for q in range(QUADS):
            nc.sync.dma_start(vss_sb[QUAD * q : QUAD * q + 4, :].bitcast(I32), vs_scales[0, 4 * q : 4 * q + 4, :].bitcast(I32))
        nc.sync.dma_start(offs4_sb[:], offs4)
        with nc.allow_non_contiguous_dma(reason="one float32 weight a row of out"):
            nc.sync.dma_start(su_sb[:], su.rearrange("(h p) o -> p h o", p=P))

        ws_words = ws_sb[:].bitcast(I32)
        nc.vector.tensor_copy(ws_words[64:128, 0 : R // 4], ws_words[0:64, R // 4 : R // 2])
        ws_dealt = held.tile([P, PACK * P], U8, name="ws_dealt", align_bytes=64)
        nc.vector.tensor_copy(ws_dealt[:].rearrange("p (t m) -> p t m", t=PACK), ws_sb[:, 0:R].rearrange("p (m t) -> p t m", t=PACK))
        w_by_slot = w_sb[:].rearrange("p (m t) -> p t m", t=PACK)
        w_dealt = []
        for t in range(PACK):
            slot = held.tile([P, P], U16, name="w_slot%d" % t, align_bytes=64)
            nc.scalar.copy(slot[:], w_by_slot[:, t, :])
            w_dealt.append(slot)

        xg_scales = held.tile([P, J], U8, name="xg_scales", align_bytes=64)
        nc.vector.tensor_copy(xg_scales[:], xs_sb[:].indirect(offs_sb[:]))
        halves = [slice(0, J // 2), slice(J // 2, J)]
        xg_words = held.tile([P, J], U32, name="xg_words", align_bytes=64)
        for cols in halves:
            nc.vector.tensor_copy(xg_words[:, cols], xt_sb[:].indirect(offs_sb[:, cols.start // 16 : cols.stop // 16]))

        vg_words = held.tile([P, U], U16, name="vg_words", align_bytes=64)
        nc.vector.tensor_copy(vg_words[:], vs_sb[:].indirect(offs3_sb[:]))

        hid = held.tile([P, PACK * O], BF16, name="hid", align_bytes=64)

        def product(t, cols, a_ps):
            nc.tensor.matmul_mx(a_ps, lhsT=w_dealt[t][:].bitcast(FP4X4), lhsT_scale=ws_dealt[:, P * t : P * (t + 1)],
                                rhs=xg_words[:, cols].bitcast(FP8X4), rhs_scale=xg_scales[:, cols], start=True, stop=True)

        for t in range(PACK):
            if t in (1, 2):
                a_sb = shared.tile([P, J], F32, name="a_sb%d" % t, offset=4 * J * (t - 1), align_bytes=64)
            else:
                a_sb = held.tile([P, J], F32, name="a_sb%d" % t, tag="a0_then_a3")
            if t == 0:
                for i, cols in enumerate(halves):
                    a_ps = psum.tile([P, J // 2], F32, name="a_ps0_%d" % i)
                    product(t, cols, a_ps[:])
                    nc.scalar.copy(a_sb[:, cols], a_ps[:])
            else:
                a_ps = psum.tile([P, J], F32, name="a_ps%d" % t)
                product(t, slice(0, J), a_ps[:])
                nc.vector.tensor_copy(a_sb[:], a_ps[:])
            nc.scalar.activation(out=hid[:, t : PACK * O : PACK], in_=a_sb[:].indirect(offs2_sb[:]), func=ACT.Exp,
                                 bias=lo_sb[:, t : t + 1], scale=sg_sb[:, t : t + 1])

        vg_scales = held.tile([P, U], U8, name="vg_scales", align_bytes=64)
        nc.vector.tensor_copy(vg_scales[:], vss_sb[:].indirect(offs3_sb[:]))

        hid_words = held.tile([P, O], U32, name="hid_words", tag="vss_then_hid_words", align_bytes=64)
        hid_scales = held.tile([P, O], U8, name="hid_scales", align_bytes=64)
        nc.vector.quantize_mx(out=hid_words[:].bitcast(FP8X4), scales=hid_scales[:], in_=hid[:])

        for h, page in enumerate(pages):
            picks = slice(P * h, P * (h + 1))
            p_ps = psum.tile([P, O], F32, name="p_ps%d" % h)
            nc.tensor.matmul_mx(p_ps[:], lhsT=vg_words[:, picks].bitcast(FP4X4), lhsT_scale=vg_scales[:, picks],
                                rhs=hid_words[:].bitcast(FP8X4), rhs_scale=hid_scales[:], start=True, stop=True)
            p_sb = held.tile([P, O], F32, name="p_sb%d" % h)
            nc.vector.tensor_copy(p_sb[:], p_ps[:])
            nc.scalar.activation(out=page[:].indirect(offs4_sb[:]), in_=p_sb[:], func=ACT.Copy, scale=su_sb[:, h, :])
            nc.sync.dma_start(out[picks, :], page[:])
